import numpy as np, ml_dtypes
CORES = [48,51,52,55]
N = 4
BF = ml_dtypes.bfloat16
def gentries(a):
    return np.ascontiguousarray(a.reshape(8, 16, -1).transpose(0, 2, 1)).reshape(8, -1)
def gtable(e):
    e = np.asarray(e); return np.ascontiguousarray(e.reshape(8, -1, 16).transpose(0, 2, 1)).reshape(128, -1).astype(np.int32)
W, O, S, D, T, RO = 3840, 192, 64, 1, 3, 3
DS = D * S; L = O + DS
H = T * (RO - 1) // 2
def parts(rng, h, q, full=False):
    th = rng.random((N, 8, W)) < rng.choice(np.array([0.2, 0.3, 0.45]), (N, 8, 1))
    th[..., :DS] = full | (rng.random((N, 8, DS)) < 0.9); th[..., W - DS:] = full | (rng.random((N, 8, DS)) < 0.85)
    rt = DS + np.argsort(rng.random((N, 8, W - DS)), axis=-1)[..., :O]
    np.put_along_axis(th, rt, True, 2)
    order = DS + np.argsort(np.where(th, 2.0, 0.0)[..., DS:] + rng.random((N, 8, W - DS)), axis=-1)
    pos = np.zeros((N, 8, W), np.int64); np.put_along_axis(pos, order, np.arange(W - DS)[None, None, :], 2)
    nv = np.maximum(W - DS - np.sum(th[..., DS:], axis=-1), 1)[..., None, None]
    p = pos[..., None] - nv; u = rng.random((N, 8, W, 16))
    deep = (rng.random((N, 8, W, 16)) < rng.choice(q, (N, 8, W, 1))) & (p > 0)
    ix = np.where(deep, nv + (u * u * u * np.maximum(p, 0)).astype(np.int64), (u * nv).astype(np.int64))
    a = np.take_along_axis(order, ix.reshape(N, 8, 16 * W), 2).reshape(N, 8, W, 16)
    a = np.where(rng.random(a.shape) < h, rng.integers(0, DS, a.shape), a)
    return th, rt, a, order, nv
def fresh(rng, th, a, r, g):
    m = DS + rng.permutation(W - 2 * DS)
    th[r, g] = True; th[r, g, m[:24]] = False
    a[r, g] = m[rng.integers(0, 24, (W, 16))]
    return a[r, g], m[24:]
def chain(x, first, cells):
    c = np.concatenate([first[None, :], cells]); x[c[:-1], 0] = c[1:]
def values(rng):
    return np.clip(rng.integers(0, 16, (N, 8, 16, W)) + rng.integers(-4, 5, (N, 8, 1, W)), 0, 15)
def pack(th, rt, a, v):
    return {"ag": np.ascontiguousarray(a.transpose(0, 1, 3, 2)).reshape(N, 128, W).astype(np.int32), "vals": np.where(th[:, :, None, :], -1, v).reshape(N, 128, W).astype(np.float32).astype(BF),
            "rts": np.stack([gtable(x) for x in rt])}
def setup_inputs(rng):
    th, rt, a, order, nv = parts(rng, rng.choice(np.array([0.01, 0.02, 0.04]), (N, 8, 1, 1)), np.array([0.0, 0.08, 0.25]))
    return pack(th, rt, a, values(rng))
def setup_inputs_room(rng):
    th, rt, a, order, nv = parts(rng, 0.0, np.array([0.0, 0.0, 0.1]), True)
    for r in range(N):
        for g in range(4):
            lanes = rng.permutation(O); at = 0
            for d in range(D):
                n = int(rng.choice(np.array([0, 1, S - 1, S])))
                if r == 0 and d == 0: n = (S, 1, 0, S - 1)[g]
                a[r, g, rt[r, g, lanes[at:at + n]], 0] = d * S + rng.permutation(S)[:n]; at += n
    q = int(rng.integers(0, N)); j = np.arange(DS); early = np.isin(j % 4, np.array([1, 2]))
    for r in range(N):
        x, m = fresh(rng, th, a, r, 4); rt[r, 4] = m[:O]; m = m[O:]; d = (q - r) % N
        if d == 0:
            chain(x, rt[r, 4], m[:O * (T + H)].reshape(T + H, O)); m = m[O * (T + H):]
            chain(x, W - DS + j, m[:DS * H].reshape(H, DS))
        elif d <= D: x[rt[r, 4, :S], 0] = (d - 1) * S + rng.permutation(S)
        x, m = fresh(rng, th, a, r, 5); rt[r, 5] = m[:O]; m = m[O:]
        c = m[:T * DS].reshape(T, DS); chain(x, rt[r, 5, :DS], c); x[c[-1], 0] = rng.permutation(DS)
        s = rt[r, 5, DS:]; y = m[T * DS:T * DS + O - DS]; k = np.arange(O - DS) % 3
        x[s[k < 2], 0] = y[k < 2]; x[y[k == 0], 0] = s[k == 0]
        x[y[k == 1], 1] = s[k == 1]; x[y[k == 1], 8] = s[k == 1]; x[s[k == 2], 1] = s[k == 2]; x[s[k == 2], 8] = s[k == 2]
        x, m = fresh(rng, th, a, r, 6); rt[r, 6] = m[:O]; m = m[O:]; th[r, 6, W - DS:] = False
        s = rt[r, 6, :DS]; c = m[:H * DS].reshape(H, DS); x[s, 0] = rng.permutation(DS); x[s, 1] = c[0]; x[s, 8] = c[0]; chain(x, c[0], c[1:])
        x, m = fresh(rng, th, a, r, 7); rt[r, 7] = m[:O]; m = m[O:]; n = DS // 2
        s = rt[r, 7, :DS]; e = W - DS + j; c = m[:T * n].reshape(T, n); m = m[T * n:]; f = m[:T * n].reshape(T, n); z = m[T * n:T * n + n]
        x[s[early], 0] = j[early]; chain(x, s[~early], c); x[c[-1], 0] = j[~early]
        chain(x, e[early], f); x[f[-1], 0] = z[j[early] // 2]; x[e[~early], 0] = z[j[~early] // 2]; x[z, 0] = z
    return pack(th, rt, a, values(rng))
def setup_inputs_crowd(rng):
    th, rt, a, order, nv = parts(rng, 0.01, np.array([0.0, 0.1]), True); n_ = np.arange(N)[:, None]
    for g in range(8):
        k = nv[:, g, :, 0] + rng.integers(0, 4, (N, O)); hot = np.take_along_axis(order[:, g], k, 1)
        if g == 1: hot = np.full((N, O), W - 1)
        if g == 2: hot[:, 1:] = rt[:, g, :-1]
        if g == 3: hot = np.where(rng.random((N, O)) < 0.5, 0, DS - 1)
        if g == 5:
            hot[:, :DS] = np.arange(DS)
            for r in range(N):
                x = a[r, g]; v0 = order[r, g, 0]
                u = order[r, g, nv[r, g, 0, 0]:]; u = u[(u < W - DS) & ~np.isin(u, rt[r, g])]; f = u[-T - 1:]
                x[np.isin(x, f)] = v0
                x[u[:4]] = np.where(x[u[:4]] >= W - DS, v0, x[u[:4]])
                x[W - DS:, 0] = f[T]; x[f[:-1], 0] = f[1:]
                hot[r, DS:] = u[rng.integers(0, 4, O - DS)]; hot[r, O - 1] = f[0]
        a[n_, g, rt[:, g], 0] = np.where((rng.random((N, O)) < 0.8) | (g == 5), hot, a[n_, g, rt[:, g], 0])
    a[:, 1, W - 1] = order[:, 1, :16]
    return pack(th, rt, a, values(rng))
def setup_inputs_halves(rng):
    th, rt, a, order, nv = parts(rng, 0.02, np.array([0.0, 0.1, 0.2]))
    o = np.argsort(rng.random((N, 8, 16, W), dtype=np.float32), axis=2); k = rng.choice(np.array([0, 7, 8, 8, 9, 9, 10, 16]), (N, 8, 1, W))
    v = np.where(o < k, rng.choice(np.array([8, 8, 15]), (N, 8, 1, W)), rng.choice(np.array([0, 7, 7]), (N, 8, 1, W)))
    a[:, 4, :, 9:] = a[:, 4, :, 8:9]; a[:, 5, :, 1:8] = a[:, 5, :, 1:2]; a[:, 6] = a[:, 6, :, 0:1]
    a[:, 7] = np.where(rng.random((N, W, 16)) < 0.1, rng.choice(np.array([0, DS - 1, DS, W - DS, W - 1]), (N, W, 16)), a[:, 7])
    return pack(th, rt, a, v)
def setup_inputs_rings(rng):
    th, rt, a, order, nv = parts(rng, 0.01, np.array([0.0, 0.1]), True); n_ = np.arange(N)[:, None]
    for g in (0, 2, 4, 6): a[n_, g, order[:, g, 1:], 0] = order[:, g, :-1]
    for g in (1, 3, 5):
        e = np.arange(0, DS, 1 if g < 4 else 2)[None, :]
        a[n_, g, W - DS + e, 0] = (e + g * S) % DS
        a[n_, g, rt[:, g, :DS], 0] = np.arange(DS)[None, :]
        x = rt[:, g, DS:DS + 8]; a[n_, g, x, 0] = x
        x = rt[:, g, DS + 8:DS + 16]; a[n_, g, x, 0] = x[:, ::-1]
    k = (DS - 1 - np.arange(DS)) % 3; n = min(DS, O - DS)
    for r in range(N):
        x, m = fresh(rng, th, a, r, 7); e = W - DS + rng.permutation(DS)
        rt[r, 7] = np.concatenate([e, m[:O - DS]]); x[m[:n], 0] = rng.permutation(DS)[:n]; m = m[O - DS:]
        x[e[k == 0], 0] = np.roll(e[k == 0], 1)
        up = e[k == 1]; chain(x, up, m[:(T - 1) * len(up)].reshape(T - 1, len(up)))
    return pack(th, rt, a, values(rng))
def setup_inputs_spread(rng):
    th, rt, a, order, nv = parts(rng, rng.choice(np.array([0.002, 0.02, 0.1]), (N, 8, 1, 1)), np.array([0.0, 0.05, 0.15, 0.5]))
    v = np.minimum((np.exp2(4 * rng.random((N, 8, 1, W))) * rng.random((N, 8, 16, W))).astype(np.int64), 15)
    return pack(th, rt, a, np.where(rng.random((N, 8, 1, W)) < 0.5, v, 15 - v))
def check_inputs(d):
    bad = []
    v = np.asarray(d["vals"]).astype(np.float32).reshape(N, 8, 16, W); r = np.stack([gentries(x) for x in d["rts"]])
    if np.min(d["ag"]) < 0 or np.max(d["ag"]) > W - 1: bad.append("range of ag")
    if not np.all((v == np.floor(v)) & (v >= -1) & (v <= 15)): bad.append("whole numbers of vals")
    if np.any(np.any(v < 0, axis=2) != np.all(v < 0, axis=2)): bad.append("thunks are -1 in all 16 rows")
    s = np.sort(r, axis=-1)
    if np.any(s[..., 1:] == s[..., :-1]): bad.append("starting cells differ")
    if np.min(r) < DS or np.max(r) > W - 1: bad.append("range of rts")
    elif not np.all(np.take_along_axis(v[:, :, 0], r.astype(np.int64), 2) == -1): bad.append("starting cells are thunks")
    return bad
def reference(ag, vals, rts):
    B = N * 8; i16 = np.arange(16)
    arg = np.stack([gentries(x) for x in ag]).reshape(B, W, 16).astype(np.int64)
    val = vals.astype(np.float32).astype(np.int16).reshape(B, 16, W)
    cur = np.full((B, L), -1, np.int64)
    cur[:, :O] = np.stack([gentries(x) for x in rts]).reshape(B, O)
    par = np.full((B, W), -1, np.int64)
    np.put_along_axis(val, cur[:, None, :O], -2, 2)
    rows = np.arange(B)[:, None]; lane = np.arange(L)[None, :]
    for rnd in range(RO):
        for step in range(T):
            act = cur >= 0; c = np.maximum(cur, 0)
            a = arg[rows, c]
            v = np.take_along_axis(val, a.reshape(B, 1, L * 16), 2).reshape(B, 16, L, 16)
            st = v[:, 0]; s = v[..., 0]; has = st[..., 0] >= 0
            many = np.sum(s >= 8, axis=1) >= 9
            need = np.where(~has[..., None], i16 == 0, np.where(many[..., None], (i16 >= 1) & (i16 < 8), i16 >= 8))
            lack = need & (st < 0); stop = np.any(lack, axis=-1); first = np.argmax(lack, axis=-1)[..., None]
            to = np.take_along_axis(a, first, 2)[..., 0]; kind = np.take_along_axis(st, first, 2)[..., 0]
            want = act & stop & (kind == -1); done = act & ~stop
            lead = np.full((B, W), L, np.int64); b, k = np.nonzero(want); np.minimum.at(lead, (b, to[b, k]), k)
            win = want & (np.take_along_axis(lead, to, 1) == lane); ent = win & (to >= DS)
            res = np.maximum(np.max(np.where(need[:, None], v, -9), axis=-1) - s, 0)
            b, k = np.nonzero(done); val[b, :, c[b, k]] = res[b, :, k]
            b, k = np.nonzero(win); val[b, :, to[b, k]] = -2
            cur = np.where(ent, to, np.where(done, np.take_along_axis(par, c, 1), cur))
            b, k = np.nonzero(ent); par[b, to[b, k]] = c[b, k]
        if rnd < RO - 1:
            old = np.array(val).reshape(N, 8, 16, W); new = np.array(old); c4 = cur.reshape(N, 8, L)
            for r in range(N):
                for d in range(1, D + 1):
                    q = (r + d) % N; lo = (d - 1) * S; e = W - DS + lo
                    asked = old[r, :, 0, lo:lo + S] == -2; ev = old[q, :, :, e:e + S]
                    home = asked & (ev[:, 0] >= 0); go = asked & (ev[:, 0] == -1)
                    new[r, :, :, lo:lo + S] = np.where(home[:, None, :], ev, old[r, :, :, lo:lo + S])
                    new[q, :, :, e:e + S] = np.where(go[:, None, :], -2, ev)
                    c4[q, :, O + lo:O + lo + S] = np.where(go, e + np.arange(S)[None, :], c4[q, :, O + lo:O + lo + S])
            val = new.reshape(B, 16, W); cur = c4.reshape(B, L)
    return {"yv": val.reshape(N, 128, W).astype(np.float32).astype(BF), "ya": np.stack([gtable(x) for x in cur.reshape(N, 8, L)]).astype(np.float32)}

from concourse.bass import DstId, RemoteDMATransfer
from concourse.mybir import AluOpType as OP, ActivationFunctionType as AF

W, OWN, NS, NL = 3840, 192, 64, 256
STEPS, ROUNDS = 3, 3
DC = 4096.0
TH, HO = 18 * DC, 19 * DC
MID = 1920
VCH = 4
CCH = 480
OUT = (128, 384, 512, 512, 512, 512, 512, 512, 256)
KA = 4
XENG = 4
DSH = (0.5, 0.5)

F32, BF, F16, I32, U16 = "float32", "bfloat16", "float16", "int32", "uint16"
SB = {
    "AG": (W + NS, I32), "RAW": (W, BF), "V": (W + NL, BF), "RT": (12, I32),
    "A": (NL, F16), "A0U": (16, U16), "LU": (32, U16), "NN": (NL, BF), "SG": (NL, BF),
    "M0": (NL, F32), "O": (NL, F32), "OU": (128, U16), "G": (2048, BF), "GS": (2048, BF), "MS": (1024, BF),
    "F": (128, F32), "SEL": (128, F16), "R": (128, BF), "B": (16, BF), "B1": (16, F32),
    "XC": (NL, F16), "XV": (16, F32), "X2": (32, F32), "QS": (NL, F32), "TA": (400, BF),
    "BA": (NL, BF), "BB": (NL, BF), "DAT": (NL, BF), "D0": (160, F32), "D1": (480, F32), "SC": (560, F32),
    "GA": (48, F32), "GG": (32, F32), "M16": (NL, BF), "DM": (NL, BF),
    "YA": (16, F32), "Y1": (16, F32), "HC": (OWN, BF),
    "LS0": (NS, BF), "LE0": (NS, BF), "LS1": (NS, BF), "LE1": (NS, BF),
    "P1": (NS, BF), "P2": (NS, BF), "P3": (NS, BF), "Q1": (NS, BF), "Q2": (NS, BF), "GT": (16, F32),
    "IC": (144, BF), "IG": (128, BF), "IH": (136, BF), "IQ": (NL, BF), "IR": (96, F32), "IS": (16, F32),
    "PI": (8, I32), "PF": (16, F32), "ZW": (48, F32),
    "PK16": (144, F16), "PKB": (144, BF), "SS16": (144, F16), "SSB": (144, BF), "DB": (136, F16), "HB": (136, F16),
    "CB": (136, BF), "XH": (256, F16), "BO": (128, BF), "TRI": (128, BF), "ID": (128, BF), "ZM": (2048, BF),
}
SCRATCH = {k: ("sbuf", [128, n], d) for k, (n, d) in SB.items()}
SCRATCH["E"] = ("sbuf", [128, 16, NL], BF)
for _b in range(8):
    SCRATCH["ps%d" % _b] = ("psum", [128, 512], F32)
NDMA = 3 + VCH + len(OUT)
SEMAPHORES = ["pe", "dve", "act", "pool", "rx0", "rx1", "tx0", "tx1"] + ["dma%d" % i for i in range(NDMA)]


def ap(name, a=0, b=None, s=1):
    return (name, a, (SB[name][0] if name in SB else 512) if b is None else b, s)


def rank_program(g, core, T, topo):
    rank = T.rank_of(core)
    if rank is None:
        return
    n_ranks = len(T.cores)
    Q = {"pe": g.tensor, "dve": g.vector, "act": g.scalar, "pool": g, "sp": g.sync}
    count = {"pe": 0, "dve": 0, "act": 0, "pool": 0}
    clock = {}
    known = {q: {} for q in Q}
    hist = {}
    ndma = [0]
    finals = []

    def X(a):
        if len(a) > 4:
            return a[4]
        return T[a[0]][:, a[1]:a[2]:a[3]] if a[3] != 1 else T[a[0]][:, a[1]:a[2]]

    def bits(a):
        if a[0].startswith("ps"):
            return -1
        if a[3] == 1:
            return ((1 << (a[2] - a[1])) - 1) << a[1]
        m = 0
        for c in range(a[1], a[2], a[3]):
            m |= 1 << c
        return m

    def wait(q, sem, v):
        if known[q].get(sem, 0) >= v:
            return
        Q[q].wait_ge(T.sem[sem], v)
        known[q][sem] = v
        for s2, v2 in clock.get((sem, v), {}).items():
            if known[q].get(s2, 0) < v2:
                known[q][s2] = v2

    def order(q, reads, writes):
        need = {}
        for a, wr in [(a, False) for a in reads] + [(a, True) for a in writes]:
            m = bits(a)
            bank = a[0].startswith("ps")
            for e in hist.get(a[0], []):
                if not e[0] & m:
                    continue
                if e[3] == q:
                    if q == "pe" or not e[4] or (bank and wr):
                        continue
                elif not (wr or e[4] or bank):
                    continue
                need[e[1]] = max(need.get(e[1], 0), e[2])
        for sem in sorted(need, key=lambda s: s == q):
            wait(q, sem, need[sem])

    def note(q, who, sem, v, reads, writes):
        clock[(sem, v)] = dict(known[q])
        for a in writes:
            m = bits(a)
            hist[a[0]] = [e for e in hist.get(a[0], []) if e[0] & ~m] + [[m, sem, v, who, True]]
        for a in reads:
            m = bits(a)
            hist[a[0]] = [e for e in hist.get(a[0], []) if e[4] or e[1] != sem or e[0] & ~m] + [[m, sem, v, who, False]]

    def run(q, reads, writes, fn):
        order(q, reads, writes)
        count[q] += 1
        fn().then_inc(T.sem[q], 1)
        note(q, q, q, count[q], reads, writes)

    def aps(*xs):
        return [x for x in xs if isinstance(x, tuple)]

    def val(x):
        return X(x) if isinstance(x, tuple) else x

    def src(a, ix):
        return X(a).indirect(X(ix)) if ix else X(a)

    def ts(out, a, s1, op0, s2=None, op1=None, ix=None):
        def fn():
            if op1 is None:
                return g.vector.tensor_scalar(X(out), src(a, ix), val(s1), None, op0)
            return g.vector.tensor_scalar(X(out), src(a, ix), val(s1), val(s2), op0, op1)
        run("dve", aps(a, s1, s2, ix), [out], fn)

    def tt(out, a, b, op):
        run("dve", [a, b], [out], lambda: g.vector.tensor_tensor(X(out), X(a), X(b), op))

    def cp(out, a, ix=None, ox=None):
        run("dve", aps(a, ix, ox), [out], lambda: g.vector.tensor_copy(src(out, ox), src(a, ix)))

    def ms(out, c):
        run("dve", [], [out], lambda: g.vector.memset(X(out), c))

    def scan(out, d0, d1, op1):
        run("dve", [d0, d1], [out], lambda: g.vector.tensor_tensor_scan(X(out), X(d0), X(d1), 0.0, OP.mult, op1))

    def act(out, a, f=AF.Identity, bias=0.0, scale=1.0, ix=None):
        if f == AF.Copy:
            run("act", aps(a, ix), [out], lambda: g.scalar.activation(X(out), src(a, ix), f))
        else:
            run("act", aps(a, ix, scale, bias), [out],
                lambda: g.scalar.activation(X(out), src(a, ix), f, bias=val(bias), scale=val(scale)))

    def mm(out, w, r, start, stop):
        run("pe", [w, r], [out], lambda: g.tensor.matmul(X(out), X(w), X(r), start, stop))

    def iota(out, pat, base, cm):
        if SB[out[0]][1] == I32:
            run("pool", [], [out], lambda: g.iota(X(out), pat, base, cm))
        else:
            run("pool", [], [out], lambda: g.iota(X(out), pat, base, cm, allow_small_or_imprecise_dtypes=True))

    def dma(q, out, in_, reads, writes):
        order(q, reads, writes)
        sem = "dma%d" % ndma[0]
        ndma[0] += 1
        Q[q].dma_start(out, in_).then_inc(T.sem[sem], 16)
        note(q, "dma", sem, 16, reads, writes)
        finals.append((sem, 16))

    V = ap("V")
    CUR = ap("SC", 84, 160, 5)

    dma("sp", X(ap("RT")), T.rts[:, :], [], [ap("RT")])
    vw = W // VCH
    for i in range(VCH):
        a = ap("RAW", i * vw, (i + 1) * vw)
        dma("sp", X(a), T.vals[:, i * vw:(i + 1) * vw], [], [a])
    dma("sp", X(ap("AG", W, W + NS)), T.ag[:, W - NS:W], [], [ap("AG", W, W + NS)])
    dma("sp", X(ap("AG", 0, W)), T.ag[:, :], [], [ap("AG", 0, W)])

    iota(ap("PI", 0, 1), [[0, 1]], 0, 1)
    iota(ap("IC"), [[1, 144]], 0, 0)
    iota(ap("IR"), [[0, 6], [16, 16]], W - MID - OWN, 0)
    iota(ap("IH"), [[1, 17], [0, 8]], 0, 0)
    iota(ap("IG"), [[1, 8], [0, 16]], 0, 0)
    iota(ap("IQ"), [[0, 16], [1, 16]], 0, 0)
    iota(ap("IS"), [[16, 16]], W - MID, 0)

    def pf(i):
        return ap("PF", i, i + 1)

    def pi(i):
        return ap("PI", i, i + 1)
    ms(ap("MS"), 1.0)
    ts(pi(1), pi(0), 15, OP.bitwise_and)
    ts(pi(2), pi(0), 4, OP.arith_shift_right)
    ts(pi(3), pi(0), 3, OP.arith_shift_right, 1, OP.bitwise_and)
    ms(ap("HC"), HO)
    cp(ap("PF", 0, 4), ap("PI", 0, 4))
    ms(ap("V", W, W + NL), 0.0)
    P_, I_, G_, H_ = pf(0), pf(1), pf(2), pf(3)
    ts(pf(12), H_, 8.0, OP.mult)
    ts(pf(4), I_, 1000.0, OP.mult, P_, OP.add)
    ts(pf(6), H_, -1000.0, OP.mult, P_, OP.add)
    ts(pf(7), H_, -8.0, OP.mult, P_, OP.add)
    ts(pf(8), H_, -2.0, OP.mult, 1.0, OP.add)
    ts(pf(9), G_, 2.0, OP.mult, 1.0, OP.add)
    ts(ap("ZW", 0, 16), ap("IC", 0, 16), I_, OP.is_equal)
    ts(ap("ZW", 16, 32), ap("IC", 0, 16), I_, OP.is_lt, -2.0, OP.mult)
    ts(ap("ZW", 32, 48), ap("IC", 0, 16), pf(12), OP.is_ge)
    ts(ap("ID"), ap("IC", 0, 128), P_, OP.is_equal)
    ts(pf(7), pf(7), 8.0, OP.add)
    tt(ap("ZW", 16, 32), ap("ZW", 16, 32), ap("ZW", 32, 48), OP.mult)
    ts(ap("SC", 84, 560, 5), ap("IR"), I_, OP.add, float(W - MID), OP.max)
    tt(ap("ZW", 0, 16), ap("ZW", 0, 16), ap("ZW", 16, 32), OP.add)
    ts(ap("SC", 84, 140, 5), ap("RT"), -float(MID), OP.add)
    ts(ap("PK16"), ap("IC"), -15.0, OP.add, pf(4), OP.is_equal)
    ts(ap("LU", 16, 32), CUR, float(MID), OP.add)
    ts(ap("HB"), ap("IC", 0, 136), -1000.0, OP.add, pf(6), OP.is_equal)
    ts(ap("DB"), ap("IC", 0, 136), pf(7), OP.is_equal, pf(8), OP.mult)
    ts(ap("CB"), ap("IH"), pf(9), OP.is_equal)
    ms(ap("M0"), 0.0)

    for i in range(W // CCH):
        a, p = ap("RAW", i * CCH, (i + 1) * CCH), ap("ps%d" % (i % 4), 0, CCH)
        act(p, a, AF.Relu, 0.0, -TH)
        tt(ap("V", i * CCH, (i + 1) * CCH), a, p, OP.max)
    cp(V, ap("HC"), ox=ap("LU", 16, 28))
    for hs in range(16):
        act(ap("ZM", 128 * hs, 128 * hs + 128), ap("ID"), AF.Identity, 0.0, ap("ZW", hs, hs + 1))
    ms(ap("D0"), 1.0)
    ms(ap("MS", 0, 1024, 8), 0.0)
    ts(pf(5), G_, 16.0, OP.mult, H_, OP.add)
    ts(pf(10), H_, -1.0, OP.mult, 1.0, OP.add)
    ms(ap("D0", 0, 160, 5), 0.0)
    ts(ap("D1", 2, 80, 5), ap("IS"), I_, OP.add)
    ts(ap("D1", 1, 80, 5), ap("IS"), I_, OP.add, -1.0, OP.mult)
    ts(ap("DM"), ap("IQ"), I_, OP.not_equal, -DC, OP.mult)
    ts(ap("BO"), ap("IG"), G_, OP.is_equal)

    def late_constants():
        ts(ap("TRI"), ap("IQ", 0, 128), I_, OP.is_gt)
        ts(ap("SS16"), ap("IC"), -14.0, OP.add, pf(5), OP.is_equal)
        ts(ap("SSB"), ap("IC"), -14.0, OP.add, pf(5), OP.is_equal)
        ts(ap("XH", 0, 128), ap("IG"), G_, OP.is_equal, pf(10), OP.mult)
        ts(ap("XH", 128, 256), ap("IG"), G_, OP.is_equal, H_, OP.mult)
        tt(ap("TRI"), ap("TRI"), ap("BO"), OP.mult)
        ts(ap("M16"), ap("IQ"), 0.5, OP.is_ge)
        ms(ap("X2"), 0.0)
        ts(ap("PKB"), ap("IC"), -15.0, OP.add, pf(4), OP.is_equal)

    def resting():
        act(ap("B1"), CUR, AF.Sign, 0.5 - (W - MID))
        act(ap("B"), ap("B1"), AF.Identity, -2.5 * TH, -1.5 * TH)

    def lanes_prep(k):
        e = 160 + 80 * k
        act(ap("D1", 0, 80, 5), CUR, AF.Copy)
        act(ap("D1", 80, e, 5), ap("SC", 164, e + 80, 5), AF.Copy)
        act(ap("D1", 81, e, 5), ap("SC", 84, e, 5), AF.Identity, 0.0, -1.0)
        act(ap("D1", 82, e, 5), ap("SC", 84, e, 5), AF.Copy)
        if k:
            act(ap("D1", 163, e, 5), ap("SC", 84, e - 80, 5), AF.Identity, 0.0, -1.0)
            act(ap("D1", 164, e, 5), ap("SC", 84, e - 80, 5), AF.Copy)

    def args(n):
        nc = n // 16
        ts(ap("A", 0, n), ap("AG"), -float(MID), OP.add, ix=ap("LU", 16, 16 + nc))
        for p in range(16):
            mm(ap("ps0", 0, nc), ap("PK16", 15 - p, 143 - p), ap("A", p, n, 16), p == 0, p == 15)
        for w, o in (("DB", 0), ("HB", 1)):
            for h in range(2):
                mm(ap("ps1", o, n, 2), ap(w, 8 - 8 * h, 136 - 8 * h), ap("A", h, n, 2), h == 0, h == 1)

    def exchange(x):
        si, ex = ap("V", 0, NS), ap("V", W - NS, W)
        ls, le = ap("LS%d" % x), ap("LE%d" % x)
        order("pool", [si, ex], [])
        trs = []
        for j, (d, s_, l_) in enumerate(((1, si, ls), (-1, ex, le))):
            dst = T.cores[(rank + d) % n_ranks]
            rid, pid, _ = topo.addr(dst)
            m = 0
            for e in topo.engines(core, dst)[j * XENG:(j + 1) * XENG]:
                m |= 1 << e
            trs.append(RemoteDMATransfer(dst_ids=[DstId(rid=rid, pnc=pid)], dma_engine_mask=m,
                                         remote_sem=T.sem["rx%d" % x], src=X(s_), dst=X(l_)))
        g.remote_dma_fused(trs, local_sem=T.sem["tx%d" % x])
        note("pool", "dma", "tx%d" % x, 2 * XENG, [si, ex], [])
        hist[ls[0]] = [[-1, "rx%d" % x, 2 * XENG, "far", True]]
        hist[le[0]] = [[-1, "rx%d" % x, 2 * XENG, "far", True]]
        finals.append(("tx%d" % x, 2 * XENG))
        finals.append(("rx%d" % x, 2 * XENG))
        ts(ap("P1"), si, HO, OP.not_equal, HO, OP.mult)
        ts(ap("Q1"), ex, TH, OP.is_equal, HO, OP.mult)

    def exchange_in(x):
        si, ex = ap("V", 0, NS), ap("V", W - NS, W)
        ls, le = ap("LS%d" % x), ap("LE%d" % x)
        ts(ap("P2"), le, 16.0, OP.is_gt, HO, OP.mult)
        tt(ap("P1"), ap("P1"), le, OP.max)
        ts(ap("Q2"), ls, HO, OP.is_equal, HO, OP.mult)
        tt(ap("P3"), ap("P1"), ap("P2"), OP.max)
        tt(ap("Q1"), ap("Q1"), ap("Q2"), OP.min)
        tt(si, si, ap("P3"), OP.min)
        tt(ex, ex, ap("Q1"), OP.max)

    def guests():
        for p in range(16):
            mm(ap("ps5", 0, 4), ap("PKB", 15 - p, 143 - p), ap("Q1", p, NS, 16), p == 0, p == 15)

    def guests_in():
        ts(ap("GT", 0, 4), ap("ps5", 0, 4), 1.0, OP.is_ge, -float(NS), OP.mult)
        tt(ap("SC", 144, 160, 5), ap("SC", 144, 160, 5), ap("GT", 0, 4), OP.add)

    todo = []

    def level():
        if todo:
            o = 80 + 80 * todo.pop()
            scan(ap("SC", o, o + 80), ap("D0", 80, 160), ap("D1", o, o + 80), OP.add)

    def largest(a, b):
        scan(ap("GS", a, b), ap("MS", 0, b - a), ap("G", a, b), OP.max)

    last = STEPS * ROUNDS - 1
    args(OWN)
    late_constants()
    resting()
    for t in range(last + 1):
        n = OWN if t < STEPS else NL
        nc, pc = n // 16, n // 2
        hc = pc // 2
        after_x = t > 0 and t % STEPS == 0
        ts(ap("A0U", 0, nc), ap("ps0", 0, nc), float(MID), OP.add)
        level()
        if after_x:
            exchange_in(t // STEPS - 1)
        ts(ap("SG", 0, pc), V, 8.0, OP.is_ge, -0.5, OP.add, ix=ap("A0U", 0, nc // 2))
        act(ap("SG", pc, n), V, AF.Sign, -7.5, 1.0, ix=ap("A0U", nc // 2, nc))
        for c in range(2):
            for h in range(2):
                mm(ap("ps%d" % (3 * c), 0, hc), ap("CB", 8 - 8 * h, 136 - 8 * h), ap("SG", c * pc + h, (c + 1) * pc, 2),
                   h == 0, h == 1)
        if after_x:
            guests()
        else:
            mm(ap("ps4", 0, nc), ap("ID"), ap("B", 0, nc), True, False)
        mm(ap("ps7", 0, n), ap("ID"), ap("DM", 0, n), True, False)
        level()
        level()
        for c in range(2):
            ts(ap("M0", c * pc + 1, (c + 1) * pc, 2), ap("ps%d" % (3 * c), 0, hc), 0.75, OP.is_ge)
        for c in range(2):
            scan(ap("O", c * pc, (c + 1) * pc), ap("M0", c * pc, (c + 1) * pc), ap("ps1", c * pc, (c + 1) * pc), OP.add)
        for c in range(2):
            ts(ap("OU", c * hc, (c + 1) * hc), ap("O", c * pc + 1, (c + 1) * pc, 2), float(MID), OP.add)
        for c in range(2):
            c0 = c * hc
            av = hc - 2 * int(hc * DSH[c] / 2 + 0.5)
            act(ap("G", 16 * c0, 16 * (c0 + av)), V, AF.Copy, ix=ap("OU", c0, c0 + av))
            cp(ap("G", 16 * (c0 + av), 16 * (c0 + hc)), V, ix=ap("OU", c0 + av, c0 + hc))
            for hs in range(16):
                mm(ap("ps%d" % (2 + c), 0, hc), ap("ZM", 128 * hs, 128 * hs + 128),
                   ap("G", 16 * c0 + hs, 16 * (c0 + hc), 16), hs == 0, hs == 15)
        act(ap("NN", 0, n), V, AF.Relu, 15.0, -1.0, ix=ap("A0U", 0, nc))
        if after_x:
            guests_in()
            resting()
            mm(ap("ps4", 0, nc), ap("ID"), ap("B", 0, nc), True, False)
        lanes_prep(min(t + 1, last - t))
        for c in range(2):
            c0 = c * hc
            z = ap("ps%d" % (2 + c), 0, hc)
            ts(ap("F", c0, c0 + hc), z, DC, OP.is_ge)
            ts(ap("R", c0, c0 + hc), z, -16.0, OP.add, 0.0, OP.max)
            tt(ap("SEL", c0, c0 + hc), ap("F", c0, c0 + hc), ap("O", 2 * c0 + 1, 2 * (c0 + hc), 2), OP.mult)
            largest(16 * c0, 16 * hc + 8 * c0)
        for q in range(8):
            mm(ap("ps4", 0, nc), ap("SSB", 14 - 2 * q, 142 - 2 * q), ap("R", q, pc, 8), False, False)
        for h in range(2):
            mm(ap("ps5", h, n, 2), ap("XH", 128 * h, 128 * h + 128), ap("SEL", 0, pc), True, True)
        for q in range(8):
            mm(ap("ps4", 0, nc), ap("SS16", 14 - 2 * q, 142 - 2 * q), ap("SEL", q, pc, 8), False, q == 7)
        cp(ap("XC", 0, n), ap("ps5", 0, n))
        cp(ap("XV", 0, nc), ap("ps4", 0, nc))
        xv = ap("XV", 0, nc)
        big = ap("GS", 7, 8 * n, 8)
        ka = nc - (KA if nc == 16 else KA - 1)
        for k in range(ka, nc):
            act(ap("TA", 80 * (k - ka), 80 * (k - ka) + n - 16 * k), ap("ps5", 16 * k, n), AF.Abs,
                ap("XV", k, k + 1), -1.0)
        for k in range(nc):
            lo, eo = 16 * k, NL * k
            e = ("E", eo, eo + n - lo, 1, T["E"][:, k, 0:n - lo])
            if k < ka:
                ts(e, ap("XC", lo, n), ap("ps4", k, k + 1), OP.is_equal)
            else:
                act(e, ap("TA", 80 * (k - ka), 80 * (k - ka) + n - lo), AF.Relu, 1.0, -1.0)
            if k < nc - 1:
                mm(ap("ps7", lo + 16, n), ap("BO"), ("E", eo + 16, eo + n - lo, 1, T["E"][:, k, 16:n - lo]),
                   False, False)
            if k in (nc - 5, nc - 1):
                k0 = 0 if k == nc - 5 else nc - 4
                mm(ap("ps7", 16 * k0, lo + 16), ap("TRI"), ("E", NL * k0, eo + 16, 1, T["E"][:, k0:k + 1, 0:16]),
                   False, k == nc - 1)
        largest(24 * hc, 32 * hc)
        mid = (NS - 1) / 2.0
        act(ap("X2", 0, nc), xv, AF.Copy)
        act(ap("X2", 16, 16 + nc), xv, AF.Copy)
        act(ap("GA", 0, nc), xv, AF.Abs, -mid)
        act(ap("GA", 16, 48), ap("X2"), AF.Abs, TH)
        act(ap("D1", 3, 160, 5), ap("X2"), AF.Identity, 0.0, -1.0)
        act(ap("D1", 4, 160, 5), ap("X2"), AF.Copy)
        act(ap("GG", 0, nc), ap("GA", 0, nc), AF.Identity, (MID + mid + 0.5) / DC, -1.0 / DC)
        act(ap("GG", 16, 16 + nc), ap("GA", 0, nc), AF.Identity, (MID - mid - 0.5) / DC, -1.0 / DC)
        act(ap("D0", 2, 160, 5), ap("GA", 16, 48), AF.Relu, 1.0, -1.0)
        act(ap("BA", 0, n), big, AF.Abs, -TH)
        act(ap("BB", 0, n), ap("BA", 0, n), AF.Relu, DC, -1.0)
        mm(ap("ps2", 0, n), ap("ID"), ap("NN", 0, n), True, False)
        mm(ap("ps2", 0, n), ap("ID"), big, False, False)
        mm(ap("ps2", 0, n), ap("ID"), ap("BB", 0, n), False, True)
        act(ap("DAT", 0, n), ap("ps2", 0, n), AF.Relu, -15.0)
        scan(ap("QS", 0, n), ap("M16", 0, n), ap("ps7", 0, n), OP.max)
        tt(ap("D0", 4, 5 * nc, 5), ap("QS", 15, n, 16), ap("GG", 0, nc), OP.is_gt)
        tt(ap("D0", 84, 80 + 5 * nc, 5), ap("QS", 15, n, 16), ap("GG", 16, 16 + nc), OP.is_gt)
        scan(ap("SC", 0, 160), ap("D0"), ap("D1", 0, 160), OP.add)
        ts(ap("LU"), ap("SC", 4, 160, 5), float(MID), OP.add)
        todo.extend(range(1, min(t + 1, last - t) + 1))
        level()
        boundary = t % STEPS == STEPS - 1
        if not boundary:
            args(OWN if t + 1 < STEPS else NL)
            resting()
        cp(V, ap("DAT", 0, n), ox=ap("LU", 0, nc))
        if t < last and boundary:
            exchange(t // STEPS)
            args(NL)

    lo = at = 0
    for i, w in enumerate(OUT):
        a, p = ap("V", at, at + w), ap("ps%d" % (i % 4), 0, w)
        act(p, a, AF.Identity, TH / DC - 1.0, -1.0 / DC)
        tt(ap("RAW", at, at + w), a, p, OP.min)
        at += w
        if i > 0:
            dma("sp", T.yv[:, lo:at], X(ap("RAW", lo, at)), [ap("RAW", lo, at)], [])
            lo = at
        if i == 0:
            ts(ap("Y1"), CUR, float(W - MID), OP.is_ge, -2.0 * DC, OP.mult)
        if i == 1:
            tt(ap("Y1"), ap("Y1"), CUR, OP.add)
        if i == 2:
            ts(ap("YA"), ap("Y1"), float(MID), OP.add, -1.0, OP.max)
            dma("sp", T.ya[:, :], X(ap("YA")), [ap("YA")], [])
    for sem, v in finals + [(q, count[q]) for q in count]:
        wait("pool", sem, v)
